import numpy as np
import ml_dtypes


def mxq(x, axis, fmt="e4m3"):
    dtype, down = {"e4m3": (ml_dtypes.float8_e4m3fn, 7), "e5m2": (ml_dtypes.float8_e5m2, 14)}[fmt]
    v = np.moveaxis(np.asarray(x, np.float32).astype(ml_dtypes.bfloat16).astype(np.float64), axis, -1)
    blocks = v.reshape(v.shape[:-1] + (-1, 32))
    amax = np.abs(blocks).max(-1, keepdims=True)
    byte = np.maximum(np.where(amax > 0, np.frexp(amax)[1] - 1 + 127, 0) - down, 1)
    scale = np.exp2(byte - 127.0)
    codes = (blocks / scale).astype(np.float32).astype(dtype).astype(np.float64)
    return np.moveaxis((codes * scale).reshape(v.shape), -1, axis)


WIDE = False


def mx_kscale(k):
    if not WIDE:
        return np.ones(k)
    levels = np.array([10, -10, 5, -5, 0])
    if k % 512:
        return np.exp2(np.random.permutation(np.resize(levels, k // 32))).repeat(32)
    a = np.empty((k // 512, 16))
    for p in range(k // 512):
        a[p, :8] = np.random.permutation(np.resize(levels, 8))
        for g in range(8):
            far = levels[np.abs(levels - a[p, g]) >= 10]
            a[p, g + 8] = far[np.random.randint(len(far))]
    return np.exp2(a.ravel()).repeat(32)


BF16 = ml_dtypes.bfloat16


def bf(x):
    return np.asarray(x, np.float32).astype(BF16)


def f64(x):
    return np.asarray(x).astype(np.float64)

def planes(Y):
    n, m = Y.shape
    b = f64(bf(Y)).reshape(n // 32, 32, m)
    amax = np.abs(b).max(1)
    byte = np.clip(np.where(amax > 0, np.frexp(amax)[1] - 1 + 127 - 7, 1), 1, 254)
    codes = (b * np.exp2(127.0 - byte)[:, None, :]).reshape(n, m).astype(np.float32).astype(ml_dtypes.float8_e4m3fn).view(np.uint8)
    words = codes.reshape(n // 512, 128, 4, m).transpose(0, 1, 3, 2)
    return np.ascontiguousarray(words), np.ascontiguousarray(byte.astype(np.uint8).reshape(n // 512, 16, m))


DST, SRC, F = 1536, 2560, 1024

EDGE_SHARE = 0.5


def setup_inputs():
    s = mx_kscale(SRC)
    spread = np.exp(0.8 * np.random.randn(F))
    edges = np.random.rand(DST, SRC) < EDGE_SHARE
    weights = np.abs(np.random.randn(DST, SRC)) / np.sqrt(EDGE_SHARE * SRC)
    adjacency = edges * weights
    features = np.random.randn(SRC, F) * spread
    return {
        "adjacency": bf(adjacency * s[None, :]),
        "features": bf(features / s[:, None]),
        "node_scale": bf(np.exp(0.3 * np.random.randn(DST))),
        "bias": bf(0.5 * np.random.randn(F) * spread),
        "skip": bf(np.random.randn(DST, F) * spread),
    }


def reference(adjacency, features, node_scale, bias, skip):
    a = mxq(f64(adjacency), 1, "e4m3")
    h = mxq(f64(features), 0, "e4m3")
    gathered = a @ h
    active = np.maximum(f64(node_scale)[:, None] * gathered + f64(bias)[None, :], 0.0)
    y = active + f64(skip)
    words, scales = planes(y.T)
    return y, words, scales

from contextlib import ExitStack

import concourse.mybir as mybir
from concourse.masks import make_identity

DST, SRC, F = 1536, 2560, 1024
FLOPS = 2 * DST * SRC * F

F32 = mybir.dt.float32
BF16 = mybir.dt.bfloat16
I32 = mybir.dt.int32
U32 = mybir.dt.uint32
U8 = mybir.dt.uint8
FP8X4 = mybir.dt.float8_e4m3fn_x4
ALU = mybir.AluOpType

P = 128
PACK = 4
K_PASS = P * PACK
PASSES = SRC // K_PASS
TILES = DST // P
HALF = 512
HALVES = F // HALF
HEAD = 3
TURNS = ((0, 2), (2, 4), (4, 5))
A_PARTS = ((0, 1024), (1024, SRC), (0, SRC))
SPLIT = (192,192,0,448,0,448,0,448,0,384,)
ORDER = (("la",0,0,),("la",2,0,),("la",1,0,),("ta",0,0,),("la",2,1,),("ta",2,0,),("lf",0,),("lf",1,),("ta",1,0,),("da",0,0,),("da",2,0,),("qa",2,0,),("wv",0,0,),("qa",0,0,),("ta",2,1,),("ta",2,2,),("tb",),("wv",0,1,),("lh",1,),("da",1,0,),("la",1,1,),("ws",0,0,),("qh",0,0,),("qa",1,0,),("da",2,1,),("da",2,2,),("la",0,1,),("ws",0,1,),("db",),("lh",2,),("la",3,2,),("qh",0,1,),("wv",1,0,),("wv",1,1,),("lh",3,),("qa",2,1,),("mx",1,0,0,),("mx",1,1,0,),("ws",1,1,),("ta",1,1,),("ta",1,2,),("tn",),("ta",0,1,),("ta",0,2,),("da",1,2,),("da",1,1,),("da",0,1,),("da",0,2,),("dn",),("qh",1,1,),("qh",1,0,),("qa",1,1,),("mx",2,0,0,),("qa",1,2,),("mx",1,1,1,),("wv",2,1,),("wv",2,0,),("mx",0,0,0,),("mx",1,0,1,),("mx",2,0,1,),("mx",0,0,1,),("mx",0,1,0,),("mx",0,1,1,),("ta",3,0,),("qa",0,1,),("ta",3,1,),("qh",2,0,),("ws",2,1,),("qh",2,1,),("qa",0,2,),("ta",3,2,),("da",3,0,),("qa",3,0,),("mx",2,1,0,),("mx",2,0,2,),("da",3,1,),("lh",4,),("mx",2,1,1,),("mx",2,1,2,),("mx",3,0,0,),("mx",1,0,2,),("da",3,2,),("wv",3,0,),("qa",3,1,),("qh",3,0,),("wv",4,0,),("wv",3,1,),("qh",4,0,),("qa",3,2,),("la",4,2,),("mx",3,1,0,),("mx",3,1,1,),("mx",0,1,2,),("ls",0,),("la",5,2,),("ws",3,1,),("mx",3,0,1,),("mx",3,0,2,),("mx",3,0,3,),("mx",0,0,2,),("la",6,2,),("ls",3,),("mx",3,1,2,),("mx",2,0,3,),("mx",1,0,3,),("mx",1,1,2,),("mx",0,0,3,),("qh",3,1,),("wv",4,1,),("mx",0,0,4,),("mx",3,0,4,),("mx",1,0,4,),("sb",0,0,),("sb",1,0,),("sb",3,0,),("ws",4,1,),("mx",2,1,3,),("mx",1,1,3,),("mx",3,1,3,),("qa",2,2,),("ta",4,0,),("ta",4,1,),("da",4,1,),("da",4,0,),("qh",4,1,),("ta",4,2,),("mx",0,1,3,),("da",4,2,),("mx",2,0,4,),("mx",0,1,4,),("sb",0,1,),("qa",4,0,),("mx",3,1,4,),("mx",2,1,4,),("sb",2,1,),("rs",3,0,),("qa",4,1,),("sb",2,0,),("qa",4,2,),("ta",5,0,),("ta",5,1,),("da",5,0,),("ry",3,0,),("mx",4,0,0,),("mx",1,1,4,),("sb",3,1,),("rs",3,1,),("mx",4,0,1,),("la",10,2,),("la",9,2,),("ta",5,2,),("ta",6,0,),("da",5,2,),("qa",5,0,),("da",6,0,),("ta",6,1,),("qa",6,0,),("da",6,1,),("qa",6,1,),("sb",1,1,),("ta",9,0,),("ta",6,2,),("rs",0,0,),("da",9,0,),("da",6,2,),("mx",4,0,2,),("mx",4,1,0,),("mx",4,1,1,),("mx",4,1,2,),("mx",4,0,3,),("mx",4,1,3,),("mx",6,0,0,),("mx",4,0,4,),("mx",4,1,4,),("mx",6,1,0,),("mx",6,0,1,),("mx",6,1,1,),("mx",6,0,2,),("mx",6,1,2,),("ls",4,),("la",11,2,),("ls",1,),("rs",1,0,),("da",5,1,),("qa",5,1,),("qa",5,2,),("mx",6,0,3,),("mx",6,1,3,),("qa",6,2,),("la",8,2,),("ls",5,),("ls",6,),("mx",6,0,4,),("mx",5,0,0,),("rs",0,1,),("rs",1,1,),("ry",1,0,),("ry",0,0,),("ry",1,1,),("sb",6,0,),("ry",3,1,),("ls",2,),("la",7,2,),("rs",6,0,),("sb",4,0,),("mx",6,1,4,),("rs",2,0,),("sb",6,1,),("sb",4,1,),("rs",2,1,),("mx",5,0,1,),("ta",10,0,),("ta",9,1,),("ta",8,0,),("ta",8,1,),("mx",5,1,0,),("mx",5,0,2,),("mx",5,1,1,),("mx",5,0,3,),("ry",0,1,),("da",10,0,),("mx",5,1,2,),("sy",1,2,),("ls",11,),("ls",9,),("sy",0,2,),("da",8,1,),("ty",3,2,),("ta",7,0,),("da",9,1,),("da",8,0,),("dy",3,2,),("da",7,0,),("ty",0,2,),("qa",8,0,),("qa",10,0,),("qa",7,0,),("qa",8,1,),("ta",8,2,),("ta",7,1,),("da",7,1,),("mx",5,1,3,),("mx",5,0,4,),("mx",5,1,4,),("sb",5,0,),("rs",4,0,),("rs",6,1,),("qa",9,0,),("qa",7,1,),("ry",2,0,),("da",8,2,),("ry",2,1,),("ta",10,1,),("ta",7,2,),("ta",11,0,),("ta",10,2,),("da",7,2,),("dy",0,2,),("qa",8,2,),("qy",0,0,),("da",10,1,),("qy",0,1,),("ty",1,2,),("dy",1,2,),("qa",9,1,),("qa",7,2,),("rs",4,1,),("qa",10,1,),("ry",4,0,),("da",10,2,),("qy",3,0,),("rs",5,0,),("qa",10,2,),("qy",1,0,),("sy",2,2,),("ry",4,1,),("da",11,0,),("mx",7,1,0,),("sy",3,2,),("mx",7,0,0,),("mx",7,0,1,),("ry",6,0,),("mx",7,0,2,),("mx",9,1,0,),("ry",6,1,),("ls",8,),("sb",5,1,),("mx",8,0,0,),("mx",7,1,1,),("sy",6,2,),("ls",7,),("mx",8,0,1,),("mx",7,0,3,),("mx",8,0,2,),("mx",8,1,0,),("mx",7,0,4,),("sb",7,0,),("qy",3,1,),("rs",5,1,),("mx",8,1,1,),("mx",7,1,2,),("mx",9,1,1,),("mx",7,1,3,),("mx",8,0,3,),("mx",8,0,4,),("sb",8,0,),("mx",8,1,2,),("mx",8,1,3,),("mx",8,1,4,),("mx",7,1,4,),("rs",7,0,),("sb",7,1,),("ty",2,2,),("dy",2,2,),("ty",4,2,),("ta",9,2,),("ty",6,2,),("ta",11,1,),("ta",11,2,),("qa",11,0,),("qy",1,1,),("sb",8,1,),("da",9,2,),("qa",9,2,),("mx",9,0,0,),("rs",8,0,),("mx",9,0,1,),("mx",9,0,2,),("qy",2,0,),("qy",2,1,),("ry",5,0,),("da",11,1,),("ry",5,1,),("ry",7,0,),("mx",9,1,2,),("mx",9,0,3,),("mx",9,0,4,),("mx",10,1,0,),("rs",7,1,),("qa",11,1,),("mx",10,0,0,),("mx",10,0,1,),("mx",10,0,2,),("mx",10,0,3,),("mx",10,0,4,),("sb",9,0,),("dy",4,2,),("ry",8,0,),("da",11,2,),("rs",8,1,),("rs",9,0,),("ry",7,1,),("qa",11,2,),("sb",10,0,),("ls",10,),("mx",10,1,1,),("mx",9,1,3,),("mx",9,1,4,),("sb",9,1,),("dy",6,2,),("ty",5,2,),("ty",7,2,),("sy",4,2,),("rs",10,0,),("dy",7,2,),("ry",9,0,),("mx",10,1,2,),("mx",11,1,0,),("qy",6,0,),("qy",6,1,),("sy",5,2,),("sy",7,2,),("dy",5,2,),("rs",9,1,),("mx",10,1,3,),("mx",10,1,4,),("sb",10,1,),("qy",4,0,),("qy",5,0,),("qy",7,0,),("mx",11,0,0,),("mx",11,1,1,),("mx",11,0,1,),("mx",11,1,2,),("mx",11,0,2,),("mx",11,0,3,),("mx",11,0,4,),("ry",9,1,),("ry",8,1,),("sy",8,2,),("rs",10,1,),("ry",10,0,),("ry",10,1,),("sw",0,),("sy",9,2,),("ty",9,2,),("mx",11,1,3,),("mx",11,1,4,),("ty",8,2,),("qy",7,1,),("qy",5,1,),("sb",11,0,),("qy",4,1,),("ty",10,2,),("sb",11,1,),("dy",9,2,),("dy",8,2,),("rs",11,0,),("rs",11,1,),("dy",10,2,),("qy",9,0,),("qy",10,0,),("qy",10,1,),("sy",10,2,),("sw",1,),("ry",11,0,),("ry",11,1,),("ty",11,0,),("qy",8,0,),("qy",8,1,),("qy",9,1,),("ty",11,1,),("dy",11,0,),("dy",11,1,),("qy",11,0,),("qy",11,1,),("sy",11,0,),("sy",11,1,),("ss",0,),("sw",2,),("sw",3,),("ss",1,),)
PERM = (None,None,None,None,None,None,None,None,None,None,None,None,)
CAST = ("S","S","S","S","S","S","S","S","S","S","S","S","S","S","S","S","S","S","S","S","S","S","S","S",)
FAST_WEAVE = False
WORD_BATCHES = ((0, 4), (4, 8), (8, 11), (11, 12))
SCALE_BATCHES = ((0, 10), (10, 12))


def tile_sampled_graph_aggregation_g1_kernel(tc, adjacency, features, node_scale, bias, skip, out_0, out_1, out_2):
    nc = tc.nc
    with ExitStack() as ctx:
        sb = ctx.enter_context(tc.tile_pool(name="sb", bufs=1))
        ps = ctx.enter_context(tc.psum_pool(name="ps", bufs=1))

        def ring(name, count, shape, dtype):
            return [sb.tile(shape, dtype, name="%s%d" % (name, i), align_bytes=64) for i in range(count)]

        banks = [ps.tile([P, HALF], F32, name="bank%d" % i) for i in range(8)]
        ident = sb.tile([P, P], F32, name="ident")
        scale_raw = sb.tile([P, P], BF16, name="scale_raw")
        scale_rows = sb.tile([P, P], F32, name="scale_rows")
        scale_cols = sb.tile([P, TILES], F32, name="scale_cols")
        bias_raw = sb.tile([P, F // P], BF16, name="bias_raw")
        bias_all = sb.tile([P, F], BF16, name="bias_all")
        h_first = ring("h_first", HALVES, [P, PACK, HALF], BF16)
        h_raw = [None] + ring("h_raw", PASSES - 1, [P, PACK, F], BF16)
        h_codes = ring("h_codes", PASSES * HALVES, [P, HALF], U32)
        h_scales = ring("h_scales", PASSES * HALVES, [P, HALF], U8)
        slots = dict(
            bank=banks,
            woven=ring("h_woven", 4, [P, HALF, PACK], BF16),
            araw=ring("a_raw", 5, [P, SRC], BF16),
            perm=ring("a_perm", 3, [P, SRC], BF16),
            staged=ring("a_turned", 6, [P, 2 * K_PASS], BF16),
            aq=list(zip(ring("a_codes", 4, [P, PASSES * P], U32), ring("a_scales", 4, [P, PASSES * P], U8))),
            skip=ring("skips", 5, [P, F], BF16),
            aff=ring("affine", 8, [P, HALF], F32),
            y=ring("ys", 5, [P, F], F32),
            yp=ring("y_pairs", 6, [P, HALF], BF16),
            yt=ring("y_turned", 3, [P, F], BF16),
        )
        free = {kind: list(range(len(tiles))) for kind, tiles in slots.items()}
        held = {}

        def take(kind, *key):
            if (kind, key) not in held:
                held[(kind, key)] = free[kind][0]
                free[kind].remove(held[(kind, key)])
            return slots[kind][held[(kind, key)]]

        def give(kind, *key):
            free[kind].append(held[(kind, key)])

        y_codes = [sb.tile([P, HALVES, (hi - lo) * P], U32, name="y_codes%d" % lo, align_bytes=64) for lo, hi in WORD_BATCHES]
        y_scales = [sb.tile([P, HALVES, (hi - lo) * P], U8, name="y_scales%d" % lo, align_bytes=64) for lo, hi in SCALE_BATCHES]

        words_out = out_1.rearrange("g p m t -> p g (m t)").bitcast(I32)
        scales_out = out_2.rearrange("g q m -> q g m").bitcast(I32)

        ctx.enter_context(tc.manual_schedule())

        def rows(m):
            return slice(m * P, (m + 1) * P)

        def cols(h):
            return slice(h * HALF, (h + 1) * HALF)

        engine_copy = dict(V=nc.vector.tensor_copy, S=nc.scalar.copy)

        def load_a(m, part):
            lo, hi = A_PARTS[part]
            nc.sync.dma_start(out=take("araw", m)[:, lo:hi], in_=adjacency[rows(m), lo:hi])

        def h_rows(g):
            return features[g * K_PASS : (g + 1) * K_PASS, :].rearrange("(p j) f -> p j f", j=PACK)

        def load_h(g):
            nc.sync.dma_start(out=h_raw[g][:], in_=h_rows(g))

        def load_h_first(h):
            nc.sync.dma_start(out=h_first[h][:], in_=h_rows(0)[:, :, cols(h)])

        def load_skip(m):
            nc.sync.dma_start(out=take("skip", m)[:], in_=skip[rows(m), :])

        def weave(copy, g, h, lo, hi):
            src = h_first[h][:, :, lo:hi] if g == 0 else h_raw[g][:, :, h * HALF + lo : h * HALF + hi]
            dst = take("woven", g, h)[:, lo:hi, :]
            if FAST_WEAVE:
                copy(out=dst.rearrange("p (c i) j -> p c j i", i=4), in_=src.rearrange("p j (c i) -> p c j i", i=4))
            else:
                copy(out=dst, in_=src.rearrange("p j f -> p f j"))

        def quantize_h(g, h):
            i = HALVES * g + h
            nc.vector.quantize_mx(out=h_codes[i][:].bitcast(FP8X4), scales=h_scales[i][:], in_=take("woven", g, h)[:].rearrange("p f j -> p (f j)"))
            give("woven", g, h)

        def sort_a(m, j):
            lo, hi = TURNS[j]
            span = slice(lo * 2 * P, hi * 2 * P)
            engine_copy[PERM[m]](
                out=take("perm", m)[:].bitcast(F32)[:, span].rearrange("r (g u p) -> r g u p", u=2, p=P),
                in_=take("araw", m)[:].bitcast(F32)[:, span].rearrange("r (g p u) -> r g u p", u=2, p=P),
            )
            if j == len(TURNS) - 1:
                give("araw", m)

        def turn_a(m, j):
            kind = "perm" if PERM[m] else "araw"
            words = take(kind, m)[:].bitcast(F32)
            bank = take("bank", "a", m, j)
            lo, hi = TURNS[j]
            for g in range(lo, hi):
                for u in range(2):
                    at = (2 * (g - lo) + u) * P
                    if PERM[m]:
                        src = words[:, (2 * g + u) * P : (2 * g + u + 1) * P]
                    else:
                        src = words[:, 2 * P * g + u : 2 * P * (g + 1) : 2]
                    nc.tensor.transpose(bank[:, at : at + P], src, ident[:])
            if j == len(TURNS) - 1:
                give(kind, m)

        def drain_a(m, j):
            n = TURNS[j][1] - TURNS[j][0]
            dst = take("staged", m, j)[:, : n * K_PASS].bitcast(F32)
            nc.scalar.copy(
                out=dst.rearrange("p (g r u) -> p g r u", g=n, u=2),
                in_=take("bank", "a", m, j)[:, : n * 2 * P].rearrange("p (g u r) -> p g r u", g=n, u=2),
            )
            give("bank", "a", m, j)

        def quantize_a(m, j):
            lo, hi = TURNS[j]
            codes, scales = take("aq", m)
            nc.vector.quantize_mx(
                out=codes[:, lo * P : hi * P].bitcast(FP8X4),
                scales=scales[:, lo * P : hi * P],
                in_=take("staged", m, j)[:, : (hi - lo) * K_PASS],
            )
            give("staged", m, j)

        def multiply(m, h, g):
            codes, scales = take("aq", m)
            nc.tensor.matmul_mx(
                out=take("bank", "s", m, h)[:],
                lhsT=codes[:, rows(g)].bitcast(FP8X4),
                lhsT_scale=scales[:, rows(g)],
                rhs=h_codes[HALVES * g + h][:].bitcast(FP8X4),
                rhs_scale=h_scales[HALVES * g + h][:],
                start=(g == 0),
                stop=(g == PASSES - 1),
            )
            if (h, g) == (HALVES - 1, PASSES - 1):
                give("aq", m)

        def scale_and_bias(m, h):
            nc.vector.scalar_tensor_tensor(
                out=take("aff", m, h)[:], in0=take("bank", "s", m, h)[:], scalar=scale_cols[:, m : m + 1],
                in1=bias_all[:, cols(h)], op0=ALU.mult, op1=ALU.add,
            )
            give("bank", "s", m, h)

        def relu_and_skip(m, h):
            nc.vector.scalar_tensor_tensor(
                out=take("y", m)[:, cols(h)], in0=take("aff", m, h)[:], scalar=0.0,
                in1=take("skip", m)[:, cols(h)], op0=ALU.max, op1=ALU.add,
            )
            give("aff", m, h)
            if h == HALVES - 1:
                give("skip", m)

        def round_y(m, h):
            engine_copy[CAST[HALVES * m + h]](
                out=take("yp", m, h)[:].rearrange("r (u p e) -> r u p e", u=2, e=2),
                in_=take("y", m)[:, cols(h)].rearrange("r (p u e) -> r u p e", u=2, e=2),
            )

        def halves_of(which):
            return (0, 1) if which == 2 else (which,)

        def turn_y(m, which):
            bank = take("bank", "y", m, which)
            for h in halves_of(which):
                words = take("yp", m, h)[:].bitcast(F32)
                for u in range(2):
                    at = (2 * h + u) * P
                    nc.tensor.transpose(bank[:, at : at + P], words[:, u * P : (u + 1) * P], ident[:])
                give("yp", m, h)

        def drain_y(m, which):
            lo, hi = halves_of(which)[0], halves_of(which)[-1] + 1
            dst = take("yt", m)[:, lo * HALF : hi * HALF].bitcast(F32)
            nc.scalar.copy(
                out=dst.rearrange("p (g r u) -> p g r u", g=hi - lo, u=2),
                in_=take("bank", "y", m, which)[:, lo * 2 * P : hi * 2 * P].rearrange("p (g u r) -> p g r u", g=hi - lo, u=2),
            )
            give("bank", "y", m, which)

        def batch_of(batches, m):
            return [i for i, (lo, hi) in enumerate(batches) if lo <= m < hi][0]

        def quantize_y(m, h):
            wb, sc = batch_of(WORD_BATCHES, m), batch_of(SCALE_BATCHES, m)
            nc.vector.quantize_mx(
                out=y_codes[wb][:, h, rows(m - WORD_BATCHES[wb][0])].bitcast(FP8X4),
                scales=y_scales[sc][:, h, rows(m - SCALE_BATCHES[sc][0])],
                in_=take("yt", m)[:, cols(h)],
            )
            if h == HALVES - 1:
                give("yt", m)

        def store_y(m, which):
            lo, hi = halves_of(which)[0] * HALF, (halves_of(which)[-1] + 1) * HALF
            nc.sync.dma_start(out=out_0[rows(m), lo:hi], in_=take("y", m)[:, lo:hi])
            if which == 2:
                give("y", m)

        def store_words(i):
            lo, hi = WORD_BATCHES[i]
            nc.sync.dma_start(out=words_out[:, :, lo * P : hi * P], in_=y_codes[i][:].bitcast(I32))

        def store_scales(i):
            lo, hi = SCALE_BATCHES[i]
            for q in range(4):
                nc.sync.dma_start(
                    out=scales_out[4 * q : 4 * q + 4, :, lo * P // 4 : hi * P // 4],
                    in_=y_scales[i][32 * q : 32 * q + 4, :, :].bitcast(I32),
                )

        nc.scalar.dma_start(out=bias_raw[:], in_=bias.rearrange("(p j) -> p j", p=P))
        nc.scalar.dma_start(out=scale_raw[:TILES, :], in_=node_scale.rearrange("(m p) -> m p", p=P))
        make_identity(nc, ident[:])
        nc.gpsimd.memset(scale_rows[:], 0.0)
        nc.gpsimd.tensor_copy(out=scale_rows[:TILES, :], in_=scale_raw[:TILES, :])

        def turn_bias():
            bias_words = bias_raw[:].bitcast(F32)
            for j in range(4):
                nc.tensor.transpose(take("bank", "b")[:, j * P : (j + 1) * P], bias_words[:, j : j + 1].to_broadcast([P, P]), ident[:])

        def drain_bias():
            nc.scalar.copy(
                out=bias_all[:].bitcast(F32).rearrange("r (p j) -> r p j", j=4),
                in_=take("bank", "b")[:].rearrange("r (j p) -> r p j", j=4),
            )
            give("bank", "b")

        def turn_scale():
            nc.tensor.transpose(take("bank", "n")[:, :P], scale_rows[:], ident[:])

        def drain_scale():
            nc.scalar.copy(out=scale_cols[:], in_=take("bank", "n")[:, :TILES])
            give("bank", "n")

        steps = dict(
            lf=load_h_first, lh=load_h, ls=load_skip, la=load_a,
            wv=lambda g, h: weave(nc.vector.tensor_copy, g, h, SPLIT[HALVES * g + h], HALF),
            ws=lambda g, h: weave(nc.scalar.copy, g, h, 0, SPLIT[HALVES * g + h]),
            qh=quantize_h, pa=sort_a, ta=turn_a, da=drain_a, qa=quantize_a, mx=multiply, sb=scale_and_bias,
            rs=relu_and_skip, ry=round_y, ty=turn_y, dy=drain_y, qy=quantize_y,
            sy=store_y, sw=store_words, ss=store_scales,
            tb=turn_bias, db=drain_bias, tn=turn_scale, dn=drain_scale,
        )
        for step in ORDER:
            steps[step[0]](*step[1:])
